import numpy as np
import ml_dtypes


def mxq(x, axis, fmt="e4m3"):
    dtype, down = {"e4m3": (ml_dtypes.float8_e4m3fn, 7), "e5m2": (ml_dtypes.float8_e5m2, 14)}[fmt]
    v = np.moveaxis(np.asarray(x, np.float32).astype(ml_dtypes.bfloat16).astype(np.float64), axis, -1)
    blocks = v.reshape(v.shape[:-1] + (-1, 32))
    amax = np.abs(blocks).max(-1, keepdims=True)
    byte = np.maximum(np.where(amax > 0, np.frexp(amax)[1] - 1 + 127, 0) - down, 1)
    scale = np.exp2(byte - 127.0)
    codes = (blocks / scale).astype(np.float32).astype(dtype).astype(np.float64)
    return np.moveaxis((codes * scale).reshape(v.shape), -1, axis)


WIDE = False


def mx_kscale(k):
    if not WIDE:
        return np.ones(k)
    levels = np.array([30, -30])
    if k % 512:
        return np.exp2(np.random.permutation(np.resize(levels, k // 32))).repeat(32)
    a = np.empty((k // 512, 16))
    for p in range(k // 512):
        a[p, :8] = np.random.permutation(np.resize(levels, 8))
        for g in range(8):
            far = levels[np.abs(levels - a[p, g]) >= 10]
            a[p, g + 8] = far[np.random.randint(len(far))]
    return np.exp2(a.ravel()).repeat(32)


def f64(x):
    return np.asarray(x).astype(np.float64)


def striped(idx):
    return np.tile(np.asarray(idx).reshape(-1, 16).T, (8, 1)).astype(np.uint16)


def unstriped(offs):
    return offs[:16].T.reshape(-1).astype(np.int64)


E2M1 = np.array([0.0, 0.5, 1.0, 1.5, 2.0, 3.0, 4.0, 6.0, -0.0, -0.5, -1.0, -1.5, -2.0, -3.0, -4.0, -6.0])


def pack_weight(w, fmt):
    k, n = w.shape
    w = f64(np.asarray(w, np.float32).astype(ml_dtypes.bfloat16)).reshape(k // 32, 32, n)
    amax = np.abs(w).max(1)
    if fmt == "e4m3":
        byte = np.frexp(amax)[1] - 1 + 127 - 7
    else:
        mant, ex = np.frexp(amax / 6.0)
        byte = np.where(mant > 0.5, ex, ex - 1) + 127
    byte = np.clip(np.where(amax > 0, byte, 1), 1, 254)
    scaled = (w * np.exp2(127.0 - byte)[:, None, :]).reshape(k, n).astype(np.float32)
    by_word = np.ascontiguousarray(scaled.reshape(k // 512, 128, 4, n).transpose(0, 1, 3, 2))
    if fmt == "e4m3":
        words = by_word.astype(ml_dtypes.float8_e4m3fn).view(np.uint8)
    else:
        c = by_word.astype(ml_dtypes.float4_e2m1fn).view(np.uint8) & 0xF
        words = (c[..., 0::2] | (c[..., 1::2] << 4)).reshape(k // 512, 128, 2 * n)
    return np.ascontiguousarray(words), np.ascontiguousarray(byte.astype(np.uint8).reshape(k // 512, 16, n))


def unpack_weight(words, scales, fmt):
    g, _, n = scales.shape
    words = np.ascontiguousarray(words).reshape(g, 128, n, -1)
    if fmt == "e4m3":
        vals = words.view(ml_dtypes.float8_e4m3fn).astype(np.float64)
    else:
        nib = np.empty((g, 128, n, 4), np.uint8)
        nib[..., 0::2] = words & 0xF
        nib[..., 1::2] = words >> 4
        vals = E2M1[nib]
    vals = vals * np.repeat(np.exp2(scales.astype(np.float64) - 127.0), 8, axis=1)[..., None]
    return vals.transpose(0, 1, 3, 2).reshape(g * 512, n)


K, T, J, B, R, N = 512, 512, 128, 16, 512, 256


def setup_inputs():
    n = np.random.standard_normal
    idx = np.random.permutation(T)[:J]
    fk = mx_kscale(K)
    fr = mx_kscale(R)
    wp = pack_weight(n((K, R)) * 1 / np.sqrt(K) * fk[:, None] * fr, "e2m1")
    wbp = pack_weight(n((R, N)) * 1 / np.sqrt(R) / fr[:, None], "e4m3")
    return {
        "xf": (n((K, T))).astype(np.float32),
        "fk": (np.random.uniform(0.5, 2.0, (K, 1)) / fk[:, None]).astype(np.float32),
        "w_words": wp[0],
        "w_scales": wp[1],
        "us": (np.random.uniform(0.5, 2.0, (R, 1)) * fr[:, None]).astype(np.float32),
        "wb_words": wbp[0],
        "wb_scales": wbp[1],
        "rs": (1.0 * n((J, N))).astype(np.float32),
        "offs": striped(idx),
    }


def reference(xf, fk, w_words, w_scales, us, wb_words, wb_scales, rs, offs):
    idx = unstriped(offs)
    wu = unpack_weight(w_words, w_scales, "e2m1")
    wbu = unpack_weight(wb_words, wb_scales, "e4m3")
    xg = f64(xf)[:, idx]
    g1 = xg.reshape(K, B, J // B).mean(axis=2)
    g2 = np.repeat(g1, J // B, axis=1)
    u = (xg - g2) * f64(fk)
    uq = mxq(u, 0, "e4m3")
    a = wu.T @ uq
    pk1 = np.max(np.abs(a), axis=1, keepdims=True)
    hid = a / pk1 * f64(us)
    hidq = mxq(hid, 0, "e5m2")
    p = hidq.T @ wbu
    pk2 = np.max(np.abs(p), axis=1, keepdims=True)
    y = p / (pk2 + 0.2) + 0.3 * f64(rs)
    return y

@@ -1,0 +1,169 @@
+from contextlib import ExitStack
+
+import concourse.mybir as mybir
+
+F32 = mybir.dt.float32
+BF16 = mybir.dt.bfloat16
+I32 = mybir.dt.int32
+U32 = mybir.dt.uint32
+U16 = mybir.dt.uint16
+U8 = mybir.dt.uint8
+E4M3 = mybir.dt.float8_e4m3fn_x4
+E5M2 = mybir.dt.float8_e5m2_x4
+E2M1 = mybir.dt.float4_e2m1fn_x4
+ALU = mybir.AluOpType
+ACT = mybir.ActivationFunctionType
+AX = mybir.AxisListType
+
+K, T, J, R, N = 512, 512, 128, 512, 256
+P = 128
+PACK = 4
+GROUP = 8
+FLOPS = 2 * K * R * J + 2 * R * J * N
+
+
+def tile_list_centredpicks_peakscaled_rowpeaks_kernel(
+    tc, xf, fk, w_words, w_scales, us, wb_words, wb_scales, rs, offs, out
+):
+    nc = tc.nc
+    with ExitStack() as ctx:
+        sb = ctx.enter_context(tc.tile_pool(name="sb", bufs=1))
+        ps = ctx.enter_context(tc.psum_pool(name="ps", bufs=1))
+
+        w_raw = sb.tile([P, 2 * R], U8, name="w_raw", align_bytes=64)
+        nc.sync.dma_start(w_raw[:].bitcast(I32), w_words[0].bitcast(I32))
+        offsets = sb.tile([P, J // 16], U16, name="offsets")
+        nc.sync.dma_start(offsets[:], offs)
+        fk_sb = sb.tile([P, PACK], F32, name="fk_sb")
+        nc.scalar.dma_start(fk_sb[:], fk.rearrange("(p t) o -> p (t o)", t=PACK))
+        x_rows = xf.rearrange("(p t) c -> p t c", t=PACK)
+        x_plane = []
+        for t in range(PACK):
+            xt = sb.tile([P, T], F32, name="x%d" % t, align_bytes=64)
+            nc.sync.dma_start(xt[:], x_rows[:, t, :])
+            x_plane.append(xt)
+
+        ws_raw = sb.tile([P, R], U8, name="ws_raw", align_bytes=64)
+        wbs = sb.tile([P, N], U8, name="wbs", align_bytes=64)
+        nc.vector.memset(wbs[:].bitcast(U32), 0)
+        for q in range(4):
+            nc.sync.dma_start(
+                ws_raw[32 * q : 32 * (q + 1), :].bitcast(I32),
+                w_scales[0:1, 4 * q : 4 * q + 4, :].bitcast(I32).to_broadcast([8, 4, R // 4]),
+            )
+        us_sb = sb.tile([P, PACK], F32, name="us_sb")
+        nc.sync.dma_start(us_sb[:], us.rearrange("(p t) o -> p (t o)", t=PACK))
+        rs_sb = sb.tile([P, N], F32, name="rs_sb")
+        nc.sync.dma_start(rs_sb[:], rs)
+        wb = sb.tile([P, N], U32, name="wb", align_bytes=64)
+        nc.sync.dma_start(wb[:].bitcast(I32), wb_words[0].rearrange("p n t -> p (n t)").bitcast(I32))
+        for q in range(4):
+            nc.sync.dma_start(
+                wbs[32 * q : 32 * q + 4, :].bitcast(I32), wb_scales[0, 4 * q : 4 * q + 4, :].bitcast(I32)
+            )
+
+        w_dealt = sb.tile([P, 2 * R], U8, name="w_dealt", align_bytes=64)
+        nc.vector.tensor_copy(
+            w_dealt[:].bitcast(U16).rearrange("p (t c i) -> p c t i", t=PACK, i=8),
+            w_raw[:].bitcast(U16).rearrange("p (c i t) -> p c t i", t=PACK, i=8),
+        )
+        u_bf = sb.tile([P, J, PACK], BF16, name="u_bf", align_bytes=64)
+        u_codes = sb.tile([P, J], U32, name="u_codes", align_bytes=64)
+        u_scales = sb.tile([P, J], U8, name="u_scales", align_bytes=64)
+
+        def centre(t, spans):
+            xg, sums, cen = {}, {}, {}
+            for lo, hi in spans:
+                xg[lo] = sb.tile([P, hi - lo], F32, name="xg%d_%d" % (t, lo), align_bytes=64)
+                picked = x_plane[t][:].indirect(offsets[:, lo // 16 : hi // 16])
+                if hi == J:
+                    nc.scalar.activation(xg[lo][:], picked, ACT.Copy)
+                else:
+                    nc.vector.tensor_copy(xg[lo][:], picked)
+            for lo, hi in spans:
+                sums[lo] = sb.tile([P, (hi - lo) // GROUP], F32, name="sums%d_%d" % (t, lo))
+                nc.vector.tensor_reduce(sums[lo][:], xg[lo][:].rearrange("p (b i) -> p b i", i=GROUP), AX.X, ALU.add)
+            for lo, hi in spans:
+                cen[lo] = sb.tile([P, hi - lo], F32, name="cen%d_%d" % (t, lo))
+                nc.vector.scalar_tensor_tensor(
+                    cen[lo][:].rearrange("p (b i) -> p b i", i=GROUP),
+                    sums[lo][:].unsqueeze(2).to_broadcast([P, (hi - lo) // GROUP, GROUP]),
+                    -1.0 / GROUP,
+                    xg[lo][:].rearrange("p (b i) -> p b i", i=GROUP),
+                    ALU.mult,
+                    ALU.add,
+                )
+            for lo, hi in spans:
+                nc.vector.tensor_scalar(u_bf[:, lo:hi, t], cen[lo][:], fk_sb[:, t : t + 1], None, ALU.mult)
+
+        halves = [(0, J // 2), (J // 2, J)]
+        for t in range(PACK - 1):
+            centre(t, [(0, J)])
+        centre(PACK - 1, halves)
+        for lo, hi in halves:
+            nc.vector.quantize_mx(
+                u_codes[:, lo:hi].bitcast(E4M3), u_scales[:, lo:hi], u_bf[:, lo:hi, :].rearrange("p j t -> p (j t)")
+            )
+
+        ws_dealt = []
+        for t in range(PACK):
+            wst = sb.tile([P, P], U8, name="ws_dealt%d" % t, align_bytes=64)
+            nc.vector.tensor_copy(wst[:], ws_raw[:].rearrange("p (m t) -> p m t", t=PACK)[:, :, t])
+            ws_dealt.append(wst)
+
+        res = sb.tile([P, N], F32, name="res")
+        nc.scalar.activation(res[:], rs_sb[:], ACT.Copy, scale=0.3)
+
+        hid_bf = sb.tile([P, J, PACK], BF16, name="hid_bf", align_bytes=64)
+        peak = sb.tile([P, PACK], F32, name="peak")
+        inv = sb.tile([P, PACK], F32, name="inv")
+        scaled = sb.tile([P, PACK, J], F32, name="scaled")
+        for t in range(PACK):
+            a_ps = ps.tile([P, J], F32, name="a_ps%d" % t)
+            nc.tensor.matmul_mx(
+                a_ps[:],
+                lhsT=w_dealt[:, 2 * P * t : 2 * P * (t + 1)].bitcast(E2M1),
+                lhsT_scale=ws_dealt[t][:],
+                rhs=u_codes[:].bitcast(E4M3),
+                rhs_scale=u_scales[:],
+                start=True,
+                stop=True,
+            )
+            a_t = sb.tile([P, J], F32, name="a_sb%d" % t)
+            nc.scalar.copy(a_t[:], a_ps[:])
+            nc.vector.tensor_reduce(peak[:, t : t + 1], a_t[:], AX.X, ALU.max, apply_absolute_value=True)
+            nc.vector.tensor_scalar(scaled[:, t, :], a_t[:], us_sb[:, t : t + 1], None, ALU.mult)
+        nc.vector.reciprocal(inv[:], peak[:])
+        nc.vector.tensor_tensor(
+            hid_bf[:].rearrange("p (c i) t -> p c t i", i=4),
+            scaled[:].rearrange("p t (c i) -> p c t i", i=4),
+            inv[:].unsqueeze(1).unsqueeze(3).to_broadcast([P, J // 4, PACK, 4]),
+            ALU.mult,
+        )
+
+        h_codes = sb.tile([P, J], U32, name="h_codes", align_bytes=64)
+        h_scales = sb.tile([P, J], U8, name="h_scales", align_bytes=64)
+        nc.vector.quantize_mx(h_codes[:].bitcast(E5M2), h_scales[:], hid_bf[:].rearrange("p j t -> p (j t)"))
+
+        p_ps = ps.tile([P, N], F32, name="p_ps")
+        nc.tensor.matmul_mx(
+            p_ps[:],
+            lhsT=h_codes[:].bitcast(E5M2),
+            lhsT_scale=h_scales[:],
+            rhs=wb[:].bitcast(E4M3),
+            rhs_scale=wbs[:],
+            start=True,
+            stop=True,
+        )
+        p_abs = sb.tile([P, N], F32, name="p_abs")
+        nc.scalar.activation(p_abs[:], p_ps[:], ACT.Abs)
+        shifted = sb.tile([P, N], F32, name="shifted")
+        denom = sb.tile([P, 1], F32, name="denom")
+        nc.vector.tensor_scalar(shifted[:], p_abs[:], 0.2, None, ALU.add, ALU.max, accum_out=denom[:])
+        inv2 = sb.tile([P, 1], F32, name="inv2")
+        nc.vector.reciprocal(inv2[:], denom[:])
+        for h, queue in enumerate((nc.scalar, nc.sync)):
+            cols = slice(h * N // 2, (h + 1) * N // 2)
+            y = sb.tile([P, N // 2], F32, name="y%d" % h)
+            nc.vector.scalar_tensor_tensor(y[:], p_ps[:, cols], inv2[:], res[:, cols], ALU.mult, ALU.add)
+            queue.dma_start(out[:, cols], y[:])

@@ -61,6 +61,10 @@ def tile_list_centredpicks_peakscaled_rowpeaks_kernel(
             nc.sync.dma_start(
                 wbs[32 * q : 32 * q + 4, :].bitcast(I32), wb_scales[0, 4 * q : 4 * q + 4, :].bitcast(I32)
             )
+        warm_in = sb.tile([P, 1], F32, name="warm_in")
+        warm_out = sb.tile([P, 1], F32, name="warm_out")
+        nc.vector.memset(warm_in[:], 0.0)
+        nc.scalar.activation(warm_out[:], warm_in[:], ACT.Copy)
 
         w_dealt = sb.tile([P, 2 * R], U8, name="w_dealt", align_bytes=64)
         nc.vector.tensor_copy(
@@ -117,6 +121,7 @@ def tile_list_centredpicks_peakscaled_rowpeaks_kernel(
         hid_bf = sb.tile([P, J, PACK], BF16, name="hid_bf", align_bytes=64)
         peak = sb.tile([P, PACK], F32, name="peak")
         inv = sb.tile([P, PACK], F32, name="inv")
+        a_sb = []
         scaled = sb.tile([P, PACK, J], F32, name="scaled")
         for t in range(PACK):
             a_ps = ps.tile([P, J], F32, name="a_ps%d" % t)
@@ -132,8 +137,10 @@ def tile_list_centredpicks_peakscaled_rowpeaks_kernel(
             a_t = sb.tile([P, J], F32, name="a_sb%d" % t)
             nc.scalar.copy(a_t[:], a_ps[:])
             nc.vector.tensor_reduce(peak[:, t : t + 1], a_t[:], AX.X, ALU.max, apply_absolute_value=True)
-            nc.vector.tensor_scalar(scaled[:, t, :], a_t[:], us_sb[:, t : t + 1], None, ALU.mult)
+            a_sb.append(a_t)
         nc.vector.reciprocal(inv[:], peak[:])
+        for t in range(PACK):
+            nc.vector.tensor_scalar(scaled[:, t, :], a_sb[t][:], us_sb[:, t : t + 1], None, ALU.mult)
         nc.vector.tensor_tensor(
             hid_bf[:].rearrange("p (c i) t -> p c t i", i=4),
             scaled[:].rearrange("p t (c i) -> p c t i", i=4),

from contextlib import ExitStack

import concourse.mybir as mybir

F32 = mybir.dt.float32
BF16 = mybir.dt.bfloat16
I32 = mybir.dt.int32
U32 = mybir.dt.uint32
U16 = mybir.dt.uint16
U8 = mybir.dt.uint8
E4M3 = mybir.dt.float8_e4m3fn_x4
E5M2 = mybir.dt.float8_e5m2_x4
E2M1 = mybir.dt.float4_e2m1fn_x4
ALU = mybir.AluOpType
ACT = mybir.ActivationFunctionType
AX = mybir.AxisListType

K, T, J, R, N = 512, 512, 128, 512, 256
P = 128
PACK = 4
GROUP = 8
FLOPS = 2 * K * R * J + 2 * R * J * N


def tile_list_centredpicks_peakscaled_rowpeaks_kernel(
    tc, xf, fk, w_words, w_scales, us, wb_words, wb_scales, rs, offs, out
):
    nc = tc.nc
    with ExitStack() as ctx:
        sb = ctx.enter_context(tc.tile_pool(name="sb", bufs=1))
        ps = ctx.enter_context(tc.psum_pool(name="ps", bufs=1))

        w_raw = sb.tile([P, 2 * R], U8, name="w_raw", align_bytes=64)
        nc.sync.dma_start(w_raw[:].bitcast(I32), w_words[0].bitcast(I32))
        offsets = sb.tile([P, J // 16], U16, name="offsets")
        nc.sync.dma_start(offsets[:], offs)
        fk_sb = sb.tile([P, PACK], F32, name="fk_sb")
        nc.scalar.dma_start(fk_sb[:], fk.rearrange("(p t) o -> p (t o)", t=PACK))
        x_rows = xf.rearrange("(p t) c -> p t c", t=PACK)
        x_plane = []
        for t in range(PACK):
            xt = sb.tile([P, T], F32, name="x%d" % t, align_bytes=64)
            nc.sync.dma_start(xt[:], x_rows[:, t, :])
            x_plane.append(xt)

        ws_raw = sb.tile([P, R], U8, name="ws_raw", align_bytes=64)
        wbs = sb.tile([P, N], U8, name="wbs", align_bytes=64)
        nc.vector.memset(wbs[:].bitcast(U32), 0)
        for q in range(4):
            nc.sync.dma_start(
                ws_raw[32 * q : 32 * (q + 1), :].bitcast(I32),
                w_scales[0:1, 4 * q : 4 * q + 4, :].bitcast(I32).to_broadcast([8, 4, R // 4]),
            )
        us_sb = sb.tile([P, PACK], F32, name="us_sb")
        nc.sync.dma_start(us_sb[:], us.rearrange("(p t) o -> p (t o)", t=PACK))
        rs_sb = sb.tile([P, N], F32, name="rs_sb")
        nc.sync.dma_start(rs_sb[:], rs)
        wb = sb.tile([P, N], U32, name="wb", align_bytes=64)
        nc.sync.dma_start(wb[:].bitcast(I32), wb_words[0].rearrange("p n t -> p (n t)").bitcast(I32))
        for q in range(4):
            nc.sync.dma_start(
                wbs[32 * q : 32 * q + 4, :].bitcast(I32), wb_scales[0, 4 * q : 4 * q + 4, :].bitcast(I32)
            )
        warm_in = sb.tile([P, 1], F32, name="warm_in")
        warm_out = sb.tile([P, 1], F32, name="warm_out")
        nc.vector.memset(warm_in[:], 0.0)
        nc.scalar.activation(warm_out[:], warm_in[:], ACT.Copy)

        w_dealt = sb.tile([P, 2 * R], U8, name="w_dealt", align_bytes=64)
        nc.vector.tensor_copy(
            w_dealt[:].bitcast(U16).rearrange("p (t c i) -> p c t i", t=PACK, i=8),
            w_raw[:].bitcast(U16).rearrange("p (c i t) -> p c t i", t=PACK, i=8),
        )
        u_bf = sb.tile([P, J, PACK], BF16, name="u_bf", align_bytes=64)
        u_codes = sb.tile([P, J], U32, name="u_codes", align_bytes=64)
        u_scales = sb.tile([P, J], U8, name="u_scales", align_bytes=64)

        def centre(t, spans):
            xg, sums, cen = {}, {}, {}
            for lo, hi in spans:
                xg[lo] = sb.tile([P, hi - lo], F32, name="xg%d_%d" % (t, lo), align_bytes=64)
                picked = x_plane[t][:].indirect(offsets[:, lo // 16 : hi // 16])
                if hi == J:
                    nc.scalar.activation(xg[lo][:], picked, ACT.Copy)
                else:
                    nc.vector.tensor_copy(xg[lo][:], picked)
            for lo, hi in spans:
                sums[lo] = sb.tile([P, (hi - lo) // GROUP], F32, name="sums%d_%d" % (t, lo))
                nc.vector.tensor_reduce(sums[lo][:], xg[lo][:].rearrange("p (b i) -> p b i", i=GROUP), AX.X, ALU.add)
            for lo, hi in spans:
                cen[lo] = sb.tile([P, hi - lo], F32, name="cen%d_%d" % (t, lo))
                nc.vector.scalar_tensor_tensor(
                    cen[lo][:].rearrange("p (b i) -> p b i", i=GROUP),
                    sums[lo][:].unsqueeze(2).to_broadcast([P, (hi - lo) // GROUP, GROUP]),
                    -1.0 / GROUP,
                    xg[lo][:].rearrange("p (b i) -> p b i", i=GROUP),
                    ALU.mult,
                    ALU.add,
                )
            for lo, hi in spans:
                nc.vector.tensor_scalar(u_bf[:, lo:hi, t], cen[lo][:], fk_sb[:, t : t + 1], None, ALU.mult)

        halves = [(0, J // 2), (J // 2, J)]
        for t in range(PACK - 1):
            centre(t, [(0, J)])
        centre(PACK - 1, halves)
        for lo, hi in halves:
            nc.vector.quantize_mx(
                u_codes[:, lo:hi].bitcast(E4M3), u_scales[:, lo:hi], u_bf[:, lo:hi, :].rearrange("p j t -> p (j t)")
            )

        ws_dealt = []
        for t in range(PACK):
            wst = sb.tile([P, P], U8, name="ws_dealt%d" % t, align_bytes=64)
            nc.vector.tensor_copy(wst[:], ws_raw[:].rearrange("p (m t) -> p m t", t=PACK)[:, :, t])
            ws_dealt.append(wst)

        res = sb.tile([P, N], F32, name="res")
        nc.scalar.activation(res[:], rs_sb[:], ACT.Copy, scale=0.3)

        hid_bf = sb.tile([P, J, PACK], BF16, name="hid_bf", align_bytes=64)
        peak = sb.tile([P, PACK], F32, name="peak")
        inv = sb.tile([P, PACK], F32, name="inv")
        a_sb = []
        scaled = sb.tile([P, PACK, J], F32, name="scaled")
        for t in range(PACK):
            a_ps = ps.tile([P, J], F32, name="a_ps%d" % t)
            nc.tensor.matmul_mx(
                a_ps[:],
                lhsT=w_dealt[:, 2 * P * t : 2 * P * (t + 1)].bitcast(E2M1),
                lhsT_scale=ws_dealt[t][:],
                rhs=u_codes[:].bitcast(E4M3),
                rhs_scale=u_scales[:],
                start=True,
                stop=True,
            )
            a_t = sb.tile([P, J], F32, name="a_sb%d" % t)
            nc.scalar.copy(a_t[:], a_ps[:])
            nc.vector.tensor_reduce(peak[:, t : t + 1], a_t[:], AX.X, ALU.max, apply_absolute_value=True)
            a_sb.append(a_t)
        nc.vector.reciprocal(inv[:], peak[:])
        for t in range(PACK):
            nc.vector.tensor_scalar(scaled[:, t, :], a_sb[t][:], us_sb[:, t : t + 1], None, ALU.mult)
        nc.vector.tensor_tensor(
            hid_bf[:].rearrange("p (c i) t -> p c t i", i=4),
            scaled[:].rearrange("p t (c i) -> p c t i", i=4),
            inv[:].unsqueeze(1).unsqueeze(3).to_broadcast([P, J // 4, PACK, 4]),
            ALU.mult,
        )

        h_codes = sb.tile([P, J], U32, name="h_codes", align_bytes=64)
        h_scales = sb.tile([P, J], U8, name="h_scales", align_bytes=64)
        nc.vector.quantize_mx(h_codes[:].bitcast(E5M2), h_scales[:], hid_bf[:].rearrange("p j t -> p (j t)"))

        p_ps = ps.tile([P, N], F32, name="p_ps")
        nc.tensor.matmul_mx(
            p_ps[:],
            lhsT=h_codes[:].bitcast(E5M2),
            lhsT_scale=h_scales[:],
            rhs=wb[:].bitcast(E4M3),
            rhs_scale=wbs[:],
            start=True,
            stop=True,
        )
        p_abs = sb.tile([P, N], F32, name="p_abs")
        nc.scalar.activation(p_abs[:], p_ps[:], ACT.Abs)
        shifted = sb.tile([P, N], F32, name="shifted")
        denom = sb.tile([P, 1], F32, name="denom")
        nc.vector.tensor_scalar(shifted[:], p_abs[:], 0.2, None, ALU.add, ALU.max, accum_out=denom[:])
        inv2 = sb.tile([P, 1], F32, name="inv2")
        nc.vector.reciprocal(inv2[:], denom[:])
        for h, queue in enumerate((nc.scalar, nc.sync)):
            cols = slice(h * N // 2, (h + 1) * N // 2)
            y = sb.tile([P, N // 2], F32, name="y%d" % h)
            nc.vector.scalar_tensor_tensor(y[:], p_ps[:, cols], inv2[:], res[:, cols], ALU.mult, ALU.add)
            queue.dma_start(out[:, cols], y[:])
